import numpy as np
import ml_dtypes


def mxq(x, axis, fmt="e4m3"):
    dtype, down = {"e4m3": (ml_dtypes.float8_e4m3fn, 7), "e5m2": (ml_dtypes.float8_e5m2, 14)}[fmt]
    v = np.moveaxis(np.asarray(x, np.float32).astype(ml_dtypes.bfloat16).astype(np.float64), axis, -1)
    blocks = v.reshape(v.shape[:-1] + (-1, 32))
    amax = np.abs(blocks).max(-1, keepdims=True)
    byte = np.maximum(np.where(amax > 0, np.frexp(amax)[1] - 1 + 127, 0) - down, 1)
    scale = np.exp2(byte - 127.0)
    codes = (blocks / scale).astype(np.float32).astype(dtype).astype(np.float64)
    return np.moveaxis((codes * scale).reshape(v.shape), -1, axis)


WIDE = False


def mx_kscale(k):
    if not WIDE:
        return np.ones(k)
    levels = np.array([10, -10, 5, -5, 0])
    if k % 512:
        return np.exp2(np.random.permutation(np.resize(levels, k // 32))).repeat(32)
    a = np.empty((k // 512, 16))
    for p in range(k // 512):
        a[p, :8] = np.random.permutation(np.resize(levels, 8))
        for g in range(8):
            far = levels[np.abs(levels - a[p, g]) >= 10]
            a[p, g + 8] = far[np.random.randint(len(far))]
    return np.exp2(a.ravel()).repeat(32)


def f64(x):
    return np.asarray(x).astype(np.float64)


def striped(idx):
    return np.tile(np.asarray(idx).reshape(-1, 16).T, (8, 1)).astype(np.uint16)


def unstriped(offs):
    return offs[:16].T.reshape(-1).astype(np.int64)


E2M1 = np.array([0.0, 0.5, 1.0, 1.5, 2.0, 3.0, 4.0, 6.0, -0.0, -0.5, -1.0, -1.5, -2.0, -3.0, -4.0, -6.0])


def pack_weight(w, fmt):
    k, n = w.shape
    w = f64(np.asarray(w, np.float32).astype(ml_dtypes.bfloat16)).reshape(k // 32, 32, n)
    amax = np.abs(w).max(1)
    if fmt == "e4m3":
        byte = np.frexp(amax)[1] - 1 + 127 - 7
    else:
        mant, ex = np.frexp(amax / 6.0)
        byte = np.where(mant > 0.5, ex, ex - 1) + 127
    byte = np.clip(np.where(amax > 0, byte, 1), 1, 254)
    scaled = (w * np.exp2(127.0 - byte)[:, None, :]).reshape(k, n).astype(np.float32)
    by_word = np.ascontiguousarray(scaled.reshape(k // 512, 128, 4, n).transpose(0, 1, 3, 2))
    if fmt == "e4m3":
        words = by_word.astype(ml_dtypes.float8_e4m3fn).view(np.uint8)
    else:
        c = by_word.astype(ml_dtypes.float4_e2m1fn).view(np.uint8) & 0xF
        words = (c[..., 0::2] | (c[..., 1::2] << 4)).reshape(k // 512, 128, 2 * n)
    return np.ascontiguousarray(words), np.ascontiguousarray(byte.astype(np.uint8).reshape(k // 512, 16, n))


def unpack_weight(words, scales, fmt):
    g, _, n = scales.shape
    words = np.ascontiguousarray(words).reshape(g, 128, n, -1)
    if fmt == "e4m3":
        vals = words.view(ml_dtypes.float8_e4m3fn).astype(np.float64)
    else:
        nib = np.empty((g, 128, n, 4), np.uint8)
        nib[..., 0::2] = words & 0xF
        nib[..., 1::2] = words >> 4
        vals = E2M1[nib]
    vals = vals * np.repeat(np.exp2(scales.astype(np.float64) - 127.0), 8, axis=1)[..., None]
    return vals.transpose(0, 1, 3, 2).reshape(g * 512, n)


def bf(x):
    return np.asarray(x, np.float32).astype(ml_dtypes.bfloat16)


def planes(Y):
    r, m = Y.shape
    b = f64(bf(Y)).reshape(r // 32, 32, m)
    amax = np.abs(b).max(1)
    byte = np.clip(np.where(amax > 0, np.frexp(amax)[1] - 1 + 127 - 7, 1), 1, 254)
    codes = (b * np.exp2(127.0 - byte)[:, None, :]).reshape(r, m).astype(np.float32).astype(ml_dtypes.float8_e4m3fn).view(np.uint8)
    words = codes.reshape(r // 512, 128, 4, m).transpose(0, 1, 3, 2)
    return np.ascontiguousarray(words), np.ascontiguousarray(byte.astype(np.uint8).reshape(r // 512, 16, m))


K, T, J, I, N = 1024, 1024, 512, 512, 512


def setup_inputs():
    n = np.random.standard_normal
    idx = np.random.permutation(T)[:J]
    idx2 = np.random.permutation(T)[:I]
    fk = mx_kscale(K)
    xqp = pack_weight(n((K, T)) / fk[:, None], "e2m1")
    wbp = pack_weight(n((K, N)) * 1 / np.sqrt(K) * fk[:, None], "e4m3")
    return {
        "xq_words": xqp[0],
        "xq_scales": xqp[1],
        "wa": (n((K, N)) * 1 / np.sqrt(K) * fk[:, None]).astype(np.float32),
        "wb_words": wbp[0],
        "wb_scales": wbp[1],
        "ga": (np.random.uniform(0.2, 0.9, (1, J))).astype(np.float32),
        "gb": (np.random.uniform(0.2, 0.9, (1, I))).astype(np.float32),
        "res": (1.0 * n((N, T))).astype(np.float32),
        "offs": striped(idx),
        "offs2": striped(idx2),
    }


def reference(xq_words, xq_scales, wa, wb_words, wb_scales, ga, gb, res, offs, offs2):
    idx = unstriped(offs)
    idx2 = unstriped(offs2)
    xqu = unpack_weight(xq_words, xq_scales, "e2m1")
    wbu = unpack_weight(wb_words, wb_scales, "e4m3")
    waq = mxq(f64(wa), 0, "e4m3")
    xqidxg = xqu[:, idx]
    p = waq.T @ xqidxg
    xqidx2g = xqu[:, idx2]
    q = wbu.T @ xqidx2g
    pw = p * f64(ga)
    qw = q * f64(gb)
    pg = np.zeros((N, T))
    pg[:, idx] = pw
    qg = np.zeros((N, T))
    qg[:, idx2] = qw
    y = np.maximum(pg, qg) + f64(res)
    words, scales = planes(y)
    return y, words, scales

@@ -1,0 +1,274 @@
+from contextlib import ExitStack
+
+import concourse.mybir as mybir
+from concourse.masks import make_identity
+
+K, T, J, N = 1024, 1024, 512, 512
+FLOPS = 2 * 2 * K * N * J
+
+F32 = mybir.dt.float32
+BF16 = mybir.dt.bfloat16
+I32 = mybir.dt.int32
+U32 = mybir.dt.uint32
+U16 = mybir.dt.uint16
+U8 = mybir.dt.uint8
+FP8X4 = mybir.dt.float8_e4m3fn_x4
+FP4X4 = mybir.dt.float4_e2m1fn_x4
+ALU = mybir.AluOpType
+ACT = mybir.ActivationFunctionType
+
+P = 128
+PACK = 4
+PASSES = K // (P * PACK)
+QUADS = 4
+B_CHUNKS = (128, 128, 256)
+SCALAR_MAX = 256
+A_ON_VECTOR = 512
+YQ = 4
+YW = T // YQ
+G_CAST = False
+G_ADD = False
+
+
+def tile_list_experts_strongest_pl_kernel(
+    tc, xq_words, xq_scales, wa, wb_words, wb_scales, ga, gb, res, offs, offs2, out_0, out_1, out_2
+):
+    nc = tc.nc
+    with ExitStack() as ctx:
+        keep = ctx.enter_context(tc.tile_pool(name="keep", bufs=1))
+        ring = ctx.enter_context(tc.tile_pool(name="ring", bufs=2))
+        psum = ctx.enter_context(tc.psum_pool(name="psum", bufs=1))
+
+        list_a = keep.tile([P, J // 16], U16, name="list_a")
+        list_b = keep.tile([P, J // 16], U16, name="list_b")
+        xs = keep.tile([P, PASSES, T], U8, name="xs", align_bytes=64)
+        xw = [keep.tile([P, T], U16, name="xw%d" % z, align_bytes=64) for z in range(PASSES)]
+        wbw_raw = keep.tile([P, PASSES, N], U32, name="wbw_raw", align_bytes=64)
+        wbs_raw = keep.tile([P, PASSES, N], U8, name="wbs_raw", align_bytes=64)
+        wbw = keep.tile([P, PASSES, N], U32, name="wbw", align_bytes=64)
+        wbs = keep.tile([P, PASSES, N], U8, name="wbs", align_bytes=64)
+        wa_raw = [keep.tile([P, PACK, N], F32, name="wa_raw%d" % z, align_bytes=64) for z in range(PASSES)]
+        wa_bf = [keep.tile([P, N * PACK], BF16, name="wa_bf%d" % z, align_bytes=64) for z in range(PASSES)]
+        waw = keep.tile([P, PASSES, N], U32, name="waw", align_bytes=64)
+        was = keep.tile([P, PASSES, N], U8, name="was", align_bytes=64)
+        gcol_a = keep.tile([P, PACK], F32, name="gcol_a")
+        gcol_b = keep.tile([P, PACK], F32, name="gcol_b")
+        g_a = keep.tile([P, J], F32, name="g_a")
+        g_b = keep.tile([P, J], F32, name="g_b")
+        ident = keep.tile([P, P], F32, name="ident")
+        res_t = [keep.tile([P, T], F32, name="res%d" % t) for t in range(PACK)]
+        page_a = [keep.tile([P, T], F32, name="page_a%d" % t) for t in range(PACK)]
+        page_b = [keep.tile([P, T], F32, name="page_b%d" % t) for t in range(PACK)]
+        y = [keep.tile([P, PACK, YW], F32, name="y%d" % q) for q in range(YQ)]
+        y_bf = [keep.tile([P, YW * PACK], BF16, name="y_bf%d" % q, align_bytes=64) for q in range(YQ)]
+        y_codes = keep.tile([P, T], U32, name="y_codes", align_bytes=64)
+        y_scales = keep.tile([P, T], U8, name="y_scales", align_bytes=64)
+
+        nc.gpsimd.memset(xs[:].rearrange("p z c -> p (z c)").bitcast(I32), 0)
+        nc.vector.memset(wbs_raw[:].rearrange("p z c -> p (z c)").bitcast(I32), 0)
+        make_identity(nc, ident[:])
+        nc.sync.dma_start(xw[0][:].bitcast(I32), xq_words[0].bitcast(I32))
+        nc.sync.dma_start(list_b[:], offs2)
+        for q in range(QUADS):
+            nc.sync.dma_start(
+                xs[32 * q : 32 * q + 4].bitcast(I32),
+                xq_scales[:, 4 * q : 4 * q + 4, :].rearrange("z r c -> r z c").bitcast(I32),
+            )
+        nc.sync.dma_start(xw[1][:].bitcast(I32), xq_words[1].bitcast(I32))
+        nc.sync.dma_start(
+            wbw_raw[:].bitcast(I32), wb_words.rearrange("z p c r -> p z (c r)").bitcast(I32)
+        )
+        for q in range(QUADS):
+            nc.sync.dma_start(
+                wbs_raw[32 * q : 32 * q + 4].bitcast(I32),
+                wb_scales[:, 4 * q : 4 * q + 4, :].rearrange("z r c -> r z c").bitcast(I32),
+            )
+        nc.sync.dma_start(gcol_b[:], gb.rearrange("o (p m) -> (o p) m", m=PACK))
+        nc.sync.dma_start(list_a[:], offs)
+        nc.sync.dma_start(gcol_a[:], ga.rearrange("o (p m) -> (o p) m", m=PACK))
+        for z in range(PASSES):
+            nc.sync.dma_start(
+                wa_raw[z][:], wa[512 * z : 512 * (z + 1), :].rearrange("(p j) c -> p j c", j=PACK)
+            )
+        res_rows = res.rearrange("(p t) c -> t p c", t=PACK)
+        out_rows = out_0.rearrange("(p t) c -> t p c", t=PACK)
+        for t in range(PACK):
+            nc.sync.dma_start(res_t[t][:], res_rows[t])
+        for t in range(PACK - 1):
+            nc.vector.memset(page_b[t][:].bitcast(I32), 0)
+        nc.gpsimd.memset(page_b[PACK - 1][:], 0.0)
+        for t in range(PACK):
+            nc.gpsimd.memset(page_a[t][:], 0.0)
+
+        def spread(gcol, g, tag):
+            bank = psum.tile([P, PACK, P], F32, name="spread", tag=tag)
+            for m in range(PACK):
+                nc.tensor.transpose(bank[:, m, :], gcol[:, m : m + 1].to_broadcast([P, P]), ident[:])
+            nc.scalar.activation(
+                g[:].rearrange("p (n m) -> p n m", m=PACK), bank[:].rearrange("p m n -> p n m"), ACT.Copy
+            )
+
+        spread(gcol_b, g_b, "bank4")
+        spread(gcol_a, g_a, "bank5")
+
+        def gather(lst, a, w):
+            cols = lst[:, a // 16 : (a + w) // 16]
+            words = []
+            scales = []
+            for z in range(PASSES):
+                gw = ring.tile([P, w], U16, name="gw", tag="gw%d" % z, align_bytes=64)
+                nc.vector.tensor_copy(gw[:], xw[z][:].indirect(cols))
+                gs = ring.tile([P, w], U8, name="gs", tag="gs%d" % z, align_bytes=64)
+                nc.vector.tensor_copy(gs[:], xs[:, z, :].indirect(cols))
+                words.append(gw)
+                scales.append(gs)
+            return words, scales
+
+        def product(out, w_words, w_scales, t, picked):
+            cols = slice(P * t, P * (t + 1))
+            for z in range(PASSES):
+                nc.tensor.matmul_mx(
+                    out=out,
+                    lhsT=w_words[:, z, cols].bitcast(FP8X4),
+                    lhsT_scale=w_scales[:, z, cols],
+                    rhs=picked[0][z][:].bitcast(FP4X4),
+                    rhs_scale=picked[1][z][:],
+                    start=(z == 0),
+                    stop=(z == PASSES - 1),
+                )
+
+        def scatter_scalar(page, lst, a, w, src):
+            for o in range(0, w, SCALAR_MAX):
+                n = min(SCALAR_MAX, w - o)
+                cols = lst[:, (a + o) // 16 : (a + o + n) // 16]
+                nc.scalar.activation(page[:].indirect(cols), src[:, o : o + n], ACT.Copy)
+
+        starts = [sum(B_CHUNKS[:c]) for c in range(len(B_CHUNKS))]
+        picked_b = [gather(list_b, starts[0], B_CHUNKS[0])]
+        nc.scalar.copy(
+            wbw[:].rearrange("p z (t m) -> p z m t", t=PACK), wbw_raw[:].rearrange("p z (m t) -> p z m t", t=PACK)
+        )
+        nc.vector.tensor_copy(
+            wbs[:].rearrange("p z (t m) -> p z m t", t=PACK), wbs_raw[:].rearrange("p z (m t) -> p z m t", t=PACK)
+        )
+        picked_b.append(gather(list_b, starts[1], B_CHUNKS[1]))
+        bank_no = 0
+        for c, w in enumerate(B_CHUNKS):
+            a = starts[c]
+            per_bank = 512 // w
+            qw = keep.tile([P, PACK, w], F32, name="qw%d" % c)
+            for t0 in range(0, PACK, per_bank):
+                bank = psum.tile([P, per_bank, w], F32, name="bank_b", tag="bank%d" % bank_no)
+                bank_no = bank_no + 1
+                for t in range(t0, t0 + per_bank):
+                    product(bank[:, t - t0, :], wbw, wbs, t, picked_b[c])
+                nc.vector.tensor_tensor(
+                    qw[:, t0 : t0 + per_bank, :],
+                    bank[:],
+                    g_b[:, a : a + w].unsqueeze(1).to_broadcast([P, per_bank, w]),
+                    ALU.mult,
+                )
+                for t in range(t0, t0 + per_bank):
+                    scatter_scalar(page_b[t], list_b, a, w, qw[:, t, :])
+            if c + 2 < len(B_CHUNKS):
+                picked_b.append(gather(list_b, starts[c + 2], B_CHUNKS[c + 2]))
+
+        def round_wa(z):
+            dst = wa_bf[z][:].rearrange("p (t m j) -> p m j t", t=PACK, j=PACK)
+            src = wa_raw[z][:].rearrange("p j (m t) -> p m j t", t=PACK)
+            if G_CAST:
+                dst = wa_bf[z][:].rearrange("p (t m j) -> p m t j", t=PACK, j=PACK)
+                src = wa_raw[z][:].rearrange("p j (m t) -> p m t j", t=PACK)
+                nc.gpsimd.tensor_scalar(dst, src, 1.0, 0.0, ALU.mult, ALU.add)
+            else:
+                nc.vector.tensor_copy(dst, src)
+
+        picked_a = gather(list_a, 0, J)
+        for z in range(PASSES):
+            round_wa(z)
+        nc.vector.quantize_mx(out=waw[:, 0, :].bitcast(FP8X4), scales=was[:, 0, :], in_=wa_bf[0][:])
+        for h in range(2):
+            cols = slice(h * N // 2, (h + 1) * N // 2)
+            nc.vector.quantize_mx(
+                out=waw[:, 1, cols].bitcast(FP8X4),
+                scales=was[:, 1, cols],
+                in_=wa_bf[1][:, h * N * PACK // 2 : (h + 1) * N * PACK // 2],
+            )
+
+        def answers_a(t):
+            bank = psum.tile([P, J], F32, name="bank_a", tag="bank%d" % (4 + t))
+            product(bank[:], waw, was, t, picked_a)
+            pw = keep.tile([P, J], F32, name="pw%d" % t)
+            if t == 0:
+                nc.scalar.copy(pw[:], bank[:])
+            else:
+                nc.vector.tensor_tensor(pw[:], bank[:], g_a[:], ALU.mult)
+            return pw
+
+        def combine_early(t):
+            top = ring.tile([P, T], F32, name="top_whole")
+            nc.vector.tensor_tensor(top[:], page_a[t][:], page_b[t][:], ALU.max)
+            for r in range(YQ):
+                rc = slice(YW * r, YW * (r + 1))
+                nc.gpsimd.tensor_tensor(y[r][:, t, :], top[:, rc], res_t[t][:, rc], ALU.add)
+                nc.sync.dma_start(out_rows[t][:, rc], y[r][:, t, :])
+
+        def combine(t, last):
+            if G_ADD and not last:
+                combine_early(t)
+                return
+            width = YW if last else 2 * YW
+            tops = []
+            for a in range(0, T, width):
+                top = ring.tile([P, width], F32, name="top", tag="top%d" % (a // width))
+                tops.append(top)
+                nc.vector.tensor_tensor(top[:], page_a[t][:, a : a + width], page_b[t][:, a : a + width], ALU.max)
+                if len(tops) % 2 == 0:
+                    for r in range((a - width) // YW, (a + width) // YW):
+                        rc = slice(YW * r, YW * (r + 1))
+                        o = YW * r % width
+                        nc.vector.tensor_tensor(
+                            y[r][:, t, :], tops[YW * r // width][:, o : o + YW], res_t[t][:, rc], ALU.add
+                        )
+                        nc.sync.dma_start(out_rows[t][:, rc], y[r][:, t, :])
+
+        pw1 = answers_a(1)
+        p0 = answers_a(0)
+        scatter_scalar(page_a[1], list_a, 0, J, pw1)
+        nc.vector.tensor_tensor(page_a[0][:].indirect(list_a[:]), p0[:], g_a[:], ALU.mult)
+        pw2 = answers_a(2)
+        scatter_scalar(page_a[2], list_a, 0, J, pw2)
+        pw3 = answers_a(3)
+        scatter_scalar(page_a[3], list_a, 0, J, pw3)
+        combine(0, False)
+        combine(1, False)
+        combine(2, False)
+        combine(3, True)
+
+        def round_y(q, c0, c1, on_scalar):
+            dst = y_bf[q][:, PACK * c0 : PACK * c1].rearrange("p (c i t) -> p c t i", i=4, t=PACK)
+            src = y[q][:, :, c0:c1].rearrange("p t (c i) -> p c t i", i=4)
+            if on_scalar:
+                nc.scalar.copy(dst, src)
+            else:
+                nc.vector.tensor_copy(dst, src)
+
+        def quantise_y(q):
+            cols = slice(YW * q, YW * (q + 1))
+            nc.vector.quantize_mx(out=y_codes[:, cols].bitcast(FP8X4), scales=y_scales[:, cols], in_=y_bf[q][:])
+
+        codes_out = out_1[0].rearrange("p c r -> p (c r)").bitcast(I32)
+        round_y(0, 0, YW, True)
+        round_y(1, 0, YW, True)
+        round_y(2, 0, YW // 2, True)
+        round_y(3, 0, YW, False)
+        round_y(2, YW // 2, YW, False)
+        quantise_y(0)
+        quantise_y(1)
+        nc.sync.dma_start(codes_out[:, 0 : T // 2], y_codes[:, 0 : T // 2].bitcast(I32))
+        quantise_y(3)
+        quantise_y(2)
+        nc.sync.dma_start(codes_out[:, T // 2 : T], y_codes[:, T // 2 : T].bitcast(I32))
+        for q in range(QUADS):
+            eng = nc.sync if q % 2 else nc.scalar
+            eng.dma_start(out_2[0, 4 * q : 4 * q + 4, :].bitcast(I32), y_scales[32 * q : 32 * q + 4, :].bitcast(I32))

@@ -21,13 +21,15 @@ P = 128
 PACK = 4
 PASSES = K // (P * PACK)
 QUADS = 4
-B_CHUNKS = (128, 128, 256)
+B_CHUNKS = (128, 128, 128, 128)
+B_SLOTS = (0, 1, 2, 0)
+A_SLOT = 2
 SCALAR_MAX = 256
-A_ON_VECTOR = 512
+A_ON_VECTOR = 320
 YQ = 4
 YW = T // YQ
-G_CAST = False
-G_ADD = False
+G_CAST = True
+G_ADD = True
 
 
 def tile_list_experts_strongest_pl_kernel(
@@ -37,28 +39,30 @@ def tile_list_experts_strongest_pl_kernel(
     with ExitStack() as ctx:
         keep = ctx.enter_context(tc.tile_pool(name="keep", bufs=1))
         ring = ctx.enter_context(tc.tile_pool(name="ring", bufs=2))
+        shared = ctx.enter_context(tc.tile_pool(name="shared", bufs=1))
         psum = ctx.enter_context(tc.psum_pool(name="psum", bufs=1))
 
         list_a = keep.tile([P, J // 16], U16, name="list_a")
         list_b = keep.tile([P, J // 16], U16, name="list_b")
         xs = keep.tile([P, PASSES, T], U8, name="xs", align_bytes=64)
         xw = [keep.tile([P, T], U16, name="xw%d" % z, align_bytes=64) for z in range(PASSES)]
-        wbw_raw = keep.tile([P, PASSES, N], U32, name="wbw_raw", align_bytes=64)
-        wbs_raw = keep.tile([P, PASSES, N], U8, name="wbs_raw", align_bytes=64)
+        xs_packed = shared.tile([P, T], U8, name="xs_packed", align_bytes=64, offset=1536)
+        plane_a1 = keep.tile([P, J], U8, name="plane_a1", align_bytes=64)
+        wbw_raw = keep.tile([P, PASSES, N], U32, name="wbw_raw", tag="hold0", align_bytes=64)
+        wbs_raw = shared.tile([P, PASSES, N], U8, name="wbs_raw", align_bytes=64, offset=0)
         wbw = keep.tile([P, PASSES, N], U32, name="wbw", align_bytes=64)
         wbs = keep.tile([P, PASSES, N], U8, name="wbs", align_bytes=64)
-        wa_raw = [keep.tile([P, PACK, N], F32, name="wa_raw%d" % z, align_bytes=64) for z in range(PASSES)]
+        wa_raw = [keep.tile([P, PACK, N], F32, name="wa_raw%d" % z, tag="wa_raw%d" % z, align_bytes=64) for z in range(PASSES)]
         wa_bf = [keep.tile([P, N * PACK], BF16, name="wa_bf%d" % z, align_bytes=64) for z in range(PASSES)]
         waw = keep.tile([P, PASSES, N], U32, name="waw", align_bytes=64)
         was = keep.tile([P, PASSES, N], U8, name="was", align_bytes=64)
         gcol_a = keep.tile([P, PACK], F32, name="gcol_a")
-        gcol_b = keep.tile([P, PACK], F32, name="gcol_b")
+        gcol_b = keep.tile([P, PACK], F32, name="gcol_b", tag="hold2", align_bytes=64)
         g_a = keep.tile([P, J], F32, name="g_a")
         g_b = keep.tile([P, J], F32, name="g_b")
         ident = keep.tile([P, P], F32, name="ident")
         res_t = [keep.tile([P, T], F32, name="res%d" % t) for t in range(PACK)]
-        page_a = [keep.tile([P, T], F32, name="page_a%d" % t) for t in range(PACK)]
-        page_b = [keep.tile([P, T], F32, name="page_b%d" % t) for t in range(PACK)]
+        page_b = [keep.tile([P, T], F32, name="page_b%d" % t) for t in range(PACK - 1)]
         y = [keep.tile([P, PACK, YW], F32, name="y%d" % q) for q in range(YQ)]
         y_bf = [keep.tile([P, YW * PACK], BF16, name="y_bf%d" % q, align_bytes=64) for q in range(YQ)]
         y_codes = keep.tile([P, T], U32, name="y_codes", align_bytes=64)
@@ -84,21 +88,28 @@ def tile_list_experts_strongest_pl_kernel(
                 wb_scales[:, 4 * q : 4 * q + 4, :].rearrange("z r c -> r z c").bitcast(I32),
             )
         nc.sync.dma_start(gcol_b[:], gb.rearrange("o (p m) -> (o p) m", m=PACK))
-        nc.sync.dma_start(list_a[:], offs)
+        wa_rows = wa.rearrange("(z p j) c -> z p j c", p=P, j=PACK)
         nc.sync.dma_start(gcol_a[:], ga.rearrange("o (p m) -> (o p) m", m=PACK))
-        for z in range(PASSES):
+        nc.sync.dma_start(wa_raw[0][:], wa_rows[0])
+        nc.sync.dma_start(list_a[:], offs)
+        nc.gpsimd.memset(xs_packed[:].bitcast(I32), 0)
+        nc.gpsimd.memset(plane_a1[:].bitcast(I32), 0)
+        for q in range(QUADS):
             nc.sync.dma_start(
-                wa_raw[z][:], wa[512 * z : 512 * (z + 1), :].rearrange("(p j) c -> p j c", j=PACK)
+                xs_packed[32 * q : 32 * q + 8].bitcast(I32), xq_scales[:, 4 * q : 4 * q + 4, :].bitcast(I32)
             )
+        nc.sync.dma_start(wa_raw[1][:], wa_rows[1])
         res_rows = res.rearrange("(p t) c -> t p c", t=PACK)
         out_rows = out_0.rearrange("(p t) c -> t p c", t=PACK)
         for t in range(PACK):
             nc.sync.dma_start(res_t[t][:], res_rows[t])
         for t in range(PACK - 1):
             nc.vector.memset(page_b[t][:].bitcast(I32), 0)
-        nc.gpsimd.memset(page_b[PACK - 1][:], 0.0)
-        for t in range(PACK):
-            nc.gpsimd.memset(page_a[t][:], 0.0)
+
+        def cleared_page(name, tag):
+            page = keep.tile([P, T], F32, name=name, tag=tag, align_bytes=64)
+            nc.gpsimd.memset(page[:], 0.0)
+            return page
 
         def spread(gcol, g, tag):
             bank = psum.tile([P, PACK, P], F32, name="spread", tag=tag)
@@ -111,14 +122,18 @@ def tile_list_experts_strongest_pl_kernel(
         spread(gcol_b, g_b, "bank4")
         spread(gcol_a, g_a, "bank5")
 
-        def gather(lst, a, w):
+        def gather(lst, a, w, slot):
             cols = lst[:, a // 16 : (a + w) // 16]
             words = []
             scales = []
             for z in range(PASSES):
-                gw = ring.tile([P, w], U16, name="gw", tag="gw%d" % z, align_bytes=64)
+                if slot == 2:
+                    gw = shared.tile([P, w], U16, name="gw2_%d" % z, align_bytes=64, offset=256 * z)
+                    gs = shared.tile([P, w], U8, name="gs2_%d" % z, align_bytes=64, offset=512 + 128 * z)
+                else:
+                    gw = keep.tile([P, w], U16, name="gw", tag="gw%d_%d" % (z, slot), align_bytes=64)
+                    gs = keep.tile([P, w], U8, name="gs", tag="gs%d_%d" % (z, slot), align_bytes=64)
                 nc.vector.tensor_copy(gw[:], xw[z][:].indirect(cols))
-                gs = ring.tile([P, w], U8, name="gs", tag="gs%d" % z, align_bytes=64)
                 nc.vector.tensor_copy(gs[:], xs[:, z, :].indirect(cols))
                 words.append(gw)
                 scales.append(gs)
@@ -144,14 +159,17 @@ def tile_list_experts_strongest_pl_kernel(
                 nc.scalar.activation(page[:].indirect(cols), src[:, o : o + n], ACT.Copy)
 
         starts = [sum(B_CHUNKS[:c]) for c in range(len(B_CHUNKS))]
-        picked_b = [gather(list_b, starts[0], B_CHUNKS[0])]
+        picked_b = [gather(list_b, starts[c], B_CHUNKS[c], B_SLOTS[c]) for c in (0, 1)]
         nc.scalar.copy(
-            wbw[:].rearrange("p z (t m) -> p z m t", t=PACK), wbw_raw[:].rearrange("p z (m t) -> p z m t", t=PACK)
+            wbw[:].rearrange("p z (t a i) -> p z a t i", t=PACK, i=4),
+            wbw_raw[:].rearrange("p z (a i t) -> p z a t i", t=PACK, i=4),
         )
         nc.vector.tensor_copy(
-            wbs[:].rearrange("p z (t m) -> p z m t", t=PACK), wbs_raw[:].rearrange("p z (m t) -> p z m t", t=PACK)
+            wbs[:].rearrange("p z (t m) -> p z t m", t=PACK), wbs_raw[:].rearrange("p z (m t) -> p z t m", t=PACK)
         )
-        picked_b.append(gather(list_b, starts[1], B_CHUNKS[1]))
+        page_b.append(cleared_page("page_b3", "hold0"))
+        page_a = [cleared_page("page_a0", "hold2")]
+        picked_b.append(gather(list_b, starts[2], B_CHUNKS[2], B_SLOTS[2]))
         bank_no = 0
         for c, w in enumerate(B_CHUNKS):
             a = starts[c]
@@ -170,8 +188,8 @@ def tile_list_experts_strongest_pl_kernel(
                 )
                 for t in range(t0, t0 + per_bank):
                     scatter_scalar(page_b[t], list_b, a, w, qw[:, t, :])
-            if c + 2 < len(B_CHUNKS):
-                picked_b.append(gather(list_b, starts[c + 2], B_CHUNKS[c + 2]))
+            if c + 3 < len(B_CHUNKS):
+                picked_b.append(gather(list_b, starts[c + 3], B_CHUNKS[c + 3], B_SLOTS[c + 3]))
 
         def round_wa(z):
             dst = wa_bf[z][:].rearrange("p (t m j) -> p m j t", t=PACK, j=PACK)
@@ -183,9 +201,23 @@ def tile_list_experts_strongest_pl_kernel(
             else:
                 nc.vector.tensor_copy(dst, src)
 
-        picked_a = gather(list_a, 0, J)
+        planes_a = shared.tile([P, J], U8, name="planes_a", align_bytes=64, offset=0)
+        nc.vector.tensor_copy(planes_a[:], xs_packed[:].indirect(list_a[:]))
+        for q in range(QUADS):
+            nc.sync.dma_start(
+                plane_a1[32 * q : 32 * q + 4].bitcast(I32), planes_a[32 * q + 4 : 32 * q + 8].bitcast(I32)
+            )
+        words_a = []
+        for z in range(PASSES):
+            gw = shared.tile([P, J], U16, name="gwa%d" % z, align_bytes=64, offset=1024 * (z + 1))
+            nc.vector.tensor_copy(gw[:], xw[z][:].indirect(list_a[:]))
+            words_a.append(gw)
+        picked_a = (words_a, [planes_a, plane_a1])
         for z in range(PASSES):
             round_wa(z)
+        page_a.append(cleared_page("page_a1", "wa_raw0"))
+        page_a.append(cleared_page("page_a2", "wa_raw1"))
+        page_a.append(page_a[0])
         nc.vector.quantize_mx(out=waw[:, 0, :].bitcast(FP8X4), scales=was[:, 0, :], in_=wa_bf[0][:])
         for h in range(2):
             cols = slice(h * N // 2, (h + 1) * N // 2)
@@ -199,24 +231,10 @@ def tile_list_experts_strongest_pl_kernel(
             bank = psum.tile([P, J], F32, name="bank_a", tag="bank%d" % (4 + t))
             product(bank[:], waw, was, t, picked_a)
             pw = keep.tile([P, J], F32, name="pw%d" % t)
-            if t == 0:
-                nc.scalar.copy(pw[:], bank[:])
-            else:
-                nc.vector.tensor_tensor(pw[:], bank[:], g_a[:], ALU.mult)
+            nc.vector.tensor_tensor(pw[:], bank[:], g_a[:], ALU.mult)
             return pw
 
-        def combine_early(t):
-            top = ring.tile([P, T], F32, name="top_whole")
-            nc.vector.tensor_tensor(top[:], page_a[t][:], page_b[t][:], ALU.max)
-            for r in range(YQ):
-                rc = slice(YW * r, YW * (r + 1))
-                nc.gpsimd.tensor_tensor(y[r][:, t, :], top[:, rc], res_t[t][:, rc], ALU.add)
-                nc.sync.dma_start(out_rows[t][:, rc], y[r][:, t, :])
-
-        def combine(t, last):
-            if G_ADD and not last:
-                combine_early(t)
-                return
+        def combine(t, last, adder):
             width = YW if last else 2 * YW
             tops = []
             for a in range(0, T, width):
@@ -227,23 +245,24 @@ def tile_list_experts_strongest_pl_kernel(
                     for r in range((a - width) // YW, (a + width) // YW):
                         rc = slice(YW * r, YW * (r + 1))
                         o = YW * r % width
-                        nc.vector.tensor_tensor(
+                        adder.tensor_tensor(
                             y[r][:, t, :], tops[YW * r // width][:, o : o + YW], res_t[t][:, rc], ALU.add
                         )
                         nc.sync.dma_start(out_rows[t][:, rc], y[r][:, t, :])
 
+        pw0 = answers_a(0)
+        nc.vector.tensor_copy(page_a[0][:].indirect(list_a[:]), pw0[:])
         pw1 = answers_a(1)
-        p0 = answers_a(0)
         scatter_scalar(page_a[1], list_a, 0, J, pw1)
-        nc.vector.tensor_tensor(page_a[0][:].indirect(list_a[:]), p0[:], g_a[:], ALU.mult)
+        combine(0, False, nc.gpsimd if G_ADD else nc.vector)
         pw2 = answers_a(2)
-        scatter_scalar(page_a[2], list_a, 0, J, pw2)
         pw3 = answers_a(3)
+        nc.vector.tensor_copy(page_a[2][:].indirect(list_a[:, 0 : A_ON_VECTOR // 16]), pw2[:, 0:A_ON_VECTOR])
+        scatter_scalar(page_a[2], list_a, A_ON_VECTOR, J - A_ON_VECTOR, pw2[:, A_ON_VECTOR:J])
         scatter_scalar(page_a[3], list_a, 0, J, pw3)
-        combine(0, False)
-        combine(1, False)
-        combine(2, False)
-        combine(3, True)
+        combine(1, False, nc.vector)
+        combine(2, False, nc.vector)
+        combine(3, True, nc.vector)
 
         def round_y(q, c0, c1, on_scalar):
             dst = y_bf[q][:, PACK * c0 : PACK * c1].rearrange("p (c i t) -> p c t i", i=4, t=PACK)

from contextlib import ExitStack

import concourse.mybir as mybir
from concourse.masks import make_identity

K, T, J, N = 1024, 1024, 512, 512
FLOPS = 2 * 2 * K * N * J

F32 = mybir.dt.float32
BF16 = mybir.dt.bfloat16
I32 = mybir.dt.int32
U32 = mybir.dt.uint32
U16 = mybir.dt.uint16
U8 = mybir.dt.uint8
FP8X4 = mybir.dt.float8_e4m3fn_x4
FP4X4 = mybir.dt.float4_e2m1fn_x4
ALU = mybir.AluOpType
ACT = mybir.ActivationFunctionType

P = 128
PACK = 4
PASSES = K // (P * PACK)
QUADS = 4
B_CHUNKS = (128, 128, 128, 128)
B_SLOTS = (0, 1, 2, 0)
A_SLOT = 2
SCALAR_MAX = 256
A_ON_VECTOR = 320
YQ = 4
YW = T // YQ
G_CAST = True
G_ADD = True


def tile_list_experts_strongest_pl_kernel(
    tc, xq_words, xq_scales, wa, wb_words, wb_scales, ga, gb, res, offs, offs2, out_0, out_1, out_2
):
    nc = tc.nc
    with ExitStack() as ctx:
        keep = ctx.enter_context(tc.tile_pool(name="keep", bufs=1))
        ring = ctx.enter_context(tc.tile_pool(name="ring", bufs=2))
        shared = ctx.enter_context(tc.tile_pool(name="shared", bufs=1))
        psum = ctx.enter_context(tc.psum_pool(name="psum", bufs=1))

        list_a = keep.tile([P, J // 16], U16, name="list_a")
        list_b = keep.tile([P, J // 16], U16, name="list_b")
        xs = keep.tile([P, PASSES, T], U8, name="xs", align_bytes=64)
        xw = [keep.tile([P, T], U16, name="xw%d" % z, align_bytes=64) for z in range(PASSES)]
        xs_packed = shared.tile([P, T], U8, name="xs_packed", align_bytes=64, offset=1536)
        plane_a1 = keep.tile([P, J], U8, name="plane_a1", align_bytes=64)
        wbw_raw = keep.tile([P, PASSES, N], U32, name="wbw_raw", tag="hold0", align_bytes=64)
        wbs_raw = shared.tile([P, PASSES, N], U8, name="wbs_raw", align_bytes=64, offset=0)
        wbw = keep.tile([P, PASSES, N], U32, name="wbw", align_bytes=64)
        wbs = keep.tile([P, PASSES, N], U8, name="wbs", align_bytes=64)
        wa_raw = [keep.tile([P, PACK, N], F32, name="wa_raw%d" % z, tag="wa_raw%d" % z, align_bytes=64) for z in range(PASSES)]
        wa_bf = [keep.tile([P, N * PACK], BF16, name="wa_bf%d" % z, align_bytes=64) for z in range(PASSES)]
        waw = keep.tile([P, PASSES, N], U32, name="waw", align_bytes=64)
        was = keep.tile([P, PASSES, N], U8, name="was", align_bytes=64)
        gcol_a = keep.tile([P, PACK], F32, name="gcol_a")
        gcol_b = keep.tile([P, PACK], F32, name="gcol_b", tag="hold2", align_bytes=64)
        g_a = keep.tile([P, J], F32, name="g_a")
        g_b = keep.tile([P, J], F32, name="g_b")
        ident = keep.tile([P, P], F32, name="ident")
        res_t = [keep.tile([P, T], F32, name="res%d" % t) for t in range(PACK)]
        page_b = [keep.tile([P, T], F32, name="page_b%d" % t) for t in range(PACK - 1)]
        y = [keep.tile([P, PACK, YW], F32, name="y%d" % q) for q in range(YQ)]
        y_bf = [keep.tile([P, YW * PACK], BF16, name="y_bf%d" % q, align_bytes=64) for q in range(YQ)]
        y_codes = keep.tile([P, T], U32, name="y_codes", align_bytes=64)
        y_scales = keep.tile([P, T], U8, name="y_scales", align_bytes=64)

        nc.gpsimd.memset(xs[:].rearrange("p z c -> p (z c)").bitcast(I32), 0)
        nc.vector.memset(wbs_raw[:].rearrange("p z c -> p (z c)").bitcast(I32), 0)
        make_identity(nc, ident[:])
        nc.sync.dma_start(xw[0][:].bitcast(I32), xq_words[0].bitcast(I32))
        nc.sync.dma_start(list_b[:], offs2)
        for q in range(QUADS):
            nc.sync.dma_start(
                xs[32 * q : 32 * q + 4].bitcast(I32),
                xq_scales[:, 4 * q : 4 * q + 4, :].rearrange("z r c -> r z c").bitcast(I32),
            )
        nc.sync.dma_start(xw[1][:].bitcast(I32), xq_words[1].bitcast(I32))
        nc.sync.dma_start(
            wbw_raw[:].bitcast(I32), wb_words.rearrange("z p c r -> p z (c r)").bitcast(I32)
        )
        for q in range(QUADS):
            nc.sync.dma_start(
                wbs_raw[32 * q : 32 * q + 4].bitcast(I32),
                wb_scales[:, 4 * q : 4 * q + 4, :].rearrange("z r c -> r z c").bitcast(I32),
            )
        nc.sync.dma_start(gcol_b[:], gb.rearrange("o (p m) -> (o p) m", m=PACK))
        wa_rows = wa.rearrange("(z p j) c -> z p j c", p=P, j=PACK)
        nc.sync.dma_start(gcol_a[:], ga.rearrange("o (p m) -> (o p) m", m=PACK))
        nc.sync.dma_start(wa_raw[0][:], wa_rows[0])
        nc.sync.dma_start(list_a[:], offs)
        nc.gpsimd.memset(xs_packed[:].bitcast(I32), 0)
        nc.gpsimd.memset(plane_a1[:].bitcast(I32), 0)
        for q in range(QUADS):
            nc.sync.dma_start(
                xs_packed[32 * q : 32 * q + 8].bitcast(I32), xq_scales[:, 4 * q : 4 * q + 4, :].bitcast(I32)
            )
        nc.sync.dma_start(wa_raw[1][:], wa_rows[1])
        res_rows = res.rearrange("(p t) c -> t p c", t=PACK)
        out_rows = out_0.rearrange("(p t) c -> t p c", t=PACK)
        for t in range(PACK):
            nc.sync.dma_start(res_t[t][:], res_rows[t])
        for t in range(PACK - 1):
            nc.vector.memset(page_b[t][:].bitcast(I32), 0)

        def cleared_page(name, tag):
            page = keep.tile([P, T], F32, name=name, tag=tag, align_bytes=64)
            nc.gpsimd.memset(page[:], 0.0)
            return page

        def spread(gcol, g, tag):
            bank = psum.tile([P, PACK, P], F32, name="spread", tag=tag)
            for m in range(PACK):
                nc.tensor.transpose(bank[:, m, :], gcol[:, m : m + 1].to_broadcast([P, P]), ident[:])
            nc.scalar.activation(
                g[:].rearrange("p (n m) -> p n m", m=PACK), bank[:].rearrange("p m n -> p n m"), ACT.Copy
            )

        spread(gcol_b, g_b, "bank4")
        spread(gcol_a, g_a, "bank5")

        def gather(lst, a, w, slot):
            cols = lst[:, a // 16 : (a + w) // 16]
            words = []
            scales = []
            for z in range(PASSES):
                if slot == 2:
                    gw = shared.tile([P, w], U16, name="gw2_%d" % z, align_bytes=64, offset=256 * z)
                    gs = shared.tile([P, w], U8, name="gs2_%d" % z, align_bytes=64, offset=512 + 128 * z)
                else:
                    gw = keep.tile([P, w], U16, name="gw", tag="gw%d_%d" % (z, slot), align_bytes=64)
                    gs = keep.tile([P, w], U8, name="gs", tag="gs%d_%d" % (z, slot), align_bytes=64)
                nc.vector.tensor_copy(gw[:], xw[z][:].indirect(cols))
                nc.vector.tensor_copy(gs[:], xs[:, z, :].indirect(cols))
                words.append(gw)
                scales.append(gs)
            return words, scales

        def product(out, w_words, w_scales, t, picked):
            cols = slice(P * t, P * (t + 1))
            for z in range(PASSES):
                nc.tensor.matmul_mx(
                    out=out,
                    lhsT=w_words[:, z, cols].bitcast(FP8X4),
                    lhsT_scale=w_scales[:, z, cols],
                    rhs=picked[0][z][:].bitcast(FP4X4),
                    rhs_scale=picked[1][z][:],
                    start=(z == 0),
                    stop=(z == PASSES - 1),
                )

        def scatter_scalar(page, lst, a, w, src):
            for o in range(0, w, SCALAR_MAX):
                n = min(SCALAR_MAX, w - o)
                cols = lst[:, (a + o) // 16 : (a + o + n) // 16]
                nc.scalar.activation(page[:].indirect(cols), src[:, o : o + n], ACT.Copy)

        starts = [sum(B_CHUNKS[:c]) for c in range(len(B_CHUNKS))]
        picked_b = [gather(list_b, starts[c], B_CHUNKS[c], B_SLOTS[c]) for c in (0, 1)]
        nc.scalar.copy(
            wbw[:].rearrange("p z (t a i) -> p z a t i", t=PACK, i=4),
            wbw_raw[:].rearrange("p z (a i t) -> p z a t i", t=PACK, i=4),
        )
        nc.vector.tensor_copy(
            wbs[:].rearrange("p z (t m) -> p z t m", t=PACK), wbs_raw[:].rearrange("p z (m t) -> p z t m", t=PACK)
        )
        page_b.append(cleared_page("page_b3", "hold0"))
        page_a = [cleared_page("page_a0", "hold2")]
        picked_b.append(gather(list_b, starts[2], B_CHUNKS[2], B_SLOTS[2]))
        bank_no = 0
        for c, w in enumerate(B_CHUNKS):
            a = starts[c]
            per_bank = 512 // w
            qw = keep.tile([P, PACK, w], F32, name="qw%d" % c)
            for t0 in range(0, PACK, per_bank):
                bank = psum.tile([P, per_bank, w], F32, name="bank_b", tag="bank%d" % bank_no)
                bank_no = bank_no + 1
                for t in range(t0, t0 + per_bank):
                    product(bank[:, t - t0, :], wbw, wbs, t, picked_b[c])
                nc.vector.tensor_tensor(
                    qw[:, t0 : t0 + per_bank, :],
                    bank[:],
                    g_b[:, a : a + w].unsqueeze(1).to_broadcast([P, per_bank, w]),
                    ALU.mult,
                )
                for t in range(t0, t0 + per_bank):
                    scatter_scalar(page_b[t], list_b, a, w, qw[:, t, :])
            if c + 3 < len(B_CHUNKS):
                picked_b.append(gather(list_b, starts[c + 3], B_CHUNKS[c + 3], B_SLOTS[c + 3]))

        def round_wa(z):
            dst = wa_bf[z][:].rearrange("p (t m j) -> p m j t", t=PACK, j=PACK)
            src = wa_raw[z][:].rearrange("p j (m t) -> p m j t", t=PACK)
            if G_CAST:
                dst = wa_bf[z][:].rearrange("p (t m j) -> p m t j", t=PACK, j=PACK)
                src = wa_raw[z][:].rearrange("p j (m t) -> p m t j", t=PACK)
                nc.gpsimd.tensor_scalar(dst, src, 1.0, 0.0, ALU.mult, ALU.add)
            else:
                nc.vector.tensor_copy(dst, src)

        planes_a = shared.tile([P, J], U8, name="planes_a", align_bytes=64, offset=0)
        nc.vector.tensor_copy(planes_a[:], xs_packed[:].indirect(list_a[:]))
        for q in range(QUADS):
            nc.sync.dma_start(
                plane_a1[32 * q : 32 * q + 4].bitcast(I32), planes_a[32 * q + 4 : 32 * q + 8].bitcast(I32)
            )
        words_a = []
        for z in range(PASSES):
            gw = shared.tile([P, J], U16, name="gwa%d" % z, align_bytes=64, offset=1024 * (z + 1))
            nc.vector.tensor_copy(gw[:], xw[z][:].indirect(list_a[:]))
            words_a.append(gw)
        picked_a = (words_a, [planes_a, plane_a1])
        for z in range(PASSES):
            round_wa(z)
        page_a.append(cleared_page("page_a1", "wa_raw0"))
        page_a.append(cleared_page("page_a2", "wa_raw1"))
        page_a.append(page_a[0])
        nc.vector.quantize_mx(out=waw[:, 0, :].bitcast(FP8X4), scales=was[:, 0, :], in_=wa_bf[0][:])
        for h in range(2):
            cols = slice(h * N // 2, (h + 1) * N // 2)
            nc.vector.quantize_mx(
                out=waw[:, 1, cols].bitcast(FP8X4),
                scales=was[:, 1, cols],
                in_=wa_bf[1][:, h * N * PACK // 2 : (h + 1) * N * PACK // 2],
            )

        def answers_a(t):
            bank = psum.tile([P, J], F32, name="bank_a", tag="bank%d" % (4 + t))
            product(bank[:], waw, was, t, picked_a)
            pw = keep.tile([P, J], F32, name="pw%d" % t)
            nc.vector.tensor_tensor(pw[:], bank[:], g_a[:], ALU.mult)
            return pw

        def combine(t, last, adder):
            width = YW if last else 2 * YW
            tops = []
            for a in range(0, T, width):
                top = ring.tile([P, width], F32, name="top", tag="top%d" % (a // width))
                tops.append(top)
                nc.vector.tensor_tensor(top[:], page_a[t][:, a : a + width], page_b[t][:, a : a + width], ALU.max)
                if len(tops) % 2 == 0:
                    for r in range((a - width) // YW, (a + width) // YW):
                        rc = slice(YW * r, YW * (r + 1))
                        o = YW * r % width
                        adder.tensor_tensor(
                            y[r][:, t, :], tops[YW * r // width][:, o : o + YW], res_t[t][:, rc], ALU.add
                        )
                        nc.sync.dma_start(out_rows[t][:, rc], y[r][:, t, :])

        pw0 = answers_a(0)
        nc.vector.tensor_copy(page_a[0][:].indirect(list_a[:]), pw0[:])
        pw1 = answers_a(1)
        scatter_scalar(page_a[1], list_a, 0, J, pw1)
        combine(0, False, nc.gpsimd if G_ADD else nc.vector)
        pw2 = answers_a(2)
        pw3 = answers_a(3)
        nc.vector.tensor_copy(page_a[2][:].indirect(list_a[:, 0 : A_ON_VECTOR // 16]), pw2[:, 0:A_ON_VECTOR])
        scatter_scalar(page_a[2], list_a, A_ON_VECTOR, J - A_ON_VECTOR, pw2[:, A_ON_VECTOR:J])
        scatter_scalar(page_a[3], list_a, 0, J, pw3)
        combine(1, False, nc.vector)
        combine(2, False, nc.vector)
        combine(3, True, nc.vector)

        def round_y(q, c0, c1, on_scalar):
            dst = y_bf[q][:, PACK * c0 : PACK * c1].rearrange("p (c i t) -> p c t i", i=4, t=PACK)
            src = y[q][:, :, c0:c1].rearrange("p t (c i) -> p c t i", i=4)
            if on_scalar:
                nc.scalar.copy(dst, src)
            else:
                nc.vector.tensor_copy(dst, src)

        def quantise_y(q):
            cols = slice(YW * q, YW * (q + 1))
            nc.vector.quantize_mx(out=y_codes[:, cols].bitcast(FP8X4), scales=y_scales[:, cols], in_=y_bf[q][:])

        codes_out = out_1[0].rearrange("p c r -> p (c r)").bitcast(I32)
        round_y(0, 0, YW, True)
        round_y(1, 0, YW, True)
        round_y(2, 0, YW // 2, True)
        round_y(3, 0, YW, False)
        round_y(2, YW // 2, YW, False)
        quantise_y(0)
        quantise_y(1)
        nc.sync.dma_start(codes_out[:, 0 : T // 2], y_codes[:, 0 : T // 2].bitcast(I32))
        quantise_y(3)
        quantise_y(2)
        nc.sync.dma_start(codes_out[:, T // 2 : T], y_codes[:, T // 2 : T].bitcast(I32))
        for q in range(QUADS):
            eng = nc.sync if q % 2 else nc.scalar
            eng.dma_start(out_2[0, 4 * q : 4 * q + 4, :].bitcast(I32), y_scales[32 * q : 32 * q + 4, :].bitcast(I32))
